import numpy as np
import ml_dtypes


def mxq(x, axis, fmt="e4m3"):
    dtype, down = {"e4m3": (ml_dtypes.float8_e4m3fn, 7), "e5m2": (ml_dtypes.float8_e5m2, 14)}[fmt]
    v = np.moveaxis(np.asarray(x, np.float32).astype(ml_dtypes.bfloat16).astype(np.float64), axis, -1)
    blocks = v.reshape(v.shape[:-1] + (-1, 32))
    amax = np.abs(blocks).max(-1, keepdims=True)
    byte = np.maximum(np.where(amax > 0, np.frexp(amax)[1] - 1 + 127, 0) - down, 1)
    scale = np.exp2(byte - 127.0)
    codes = (blocks / scale).astype(np.float32).astype(dtype).astype(np.float64)
    return np.moveaxis((codes * scale).reshape(v.shape), -1, axis)


WIDE = False


def mx_kscale(k):
    if not WIDE:
        return np.ones(k)
    levels = np.array([10, -10, 5, -5, 0])
    if k % 512:
        return np.exp2(np.random.permutation(np.resize(levels, k // 32))).repeat(32)
    a = np.empty((k // 512, 16))
    for p in range(k // 512):
        a[p, :8] = np.random.permutation(np.resize(levels, 8))
        for g in range(8):
            far = levels[np.abs(levels - a[p, g]) >= 10]
            a[p, g + 8] = far[np.random.randint(len(far))]
    return np.exp2(a.ravel()).repeat(32)


def f64(x):
    return np.asarray(x).astype(np.float64)


def striped(idx):
    return np.tile(idx.reshape(-1, 16).T, (8, 1)).astype(np.uint16)


def unstriped(offs):
    return offs[:16].T.reshape(-1).astype(np.int64)


K, T, E, C, N = 512, 512, 2, 256, 128


def by_expert(wq, xq):
    return np.concatenate([wq[e].T @ xq[:, e * C:(e + 1) * C] for e in range(E)], axis=1)


def setup_inputs():
    n = np.random.standard_normal
    s = mx_kscale(K)[:, None]
    return {
        "xT": (n((K, T)) * s).astype(np.float32),
        "w": (n((E, K, N)) / np.sqrt(K) / s[None]).astype(np.float32),
        "offs": striped(np.random.permutation(T)[:E * C]),
    }


def reference(xT, w, offs):
    idx = unstriped(offs)
    xq = mxq(f64(xT)[:, idx], 0, "e4m3")
    y = by_expert(mxq(f64(w), 1, "e4m3"), xq)
    out = np.zeros((N, T))
    out[:, idx] = y
    return out

@@ -1,0 +1,134 @@
+from contextlib import ExitStack
+
+import concourse.mybir as mybir
+
+K, T, E, C, N = 512, 512, 2, 256, 128
+FLOPS = 2 * K * N * E * C
+
+F32 = mybir.dt.float32
+BF16 = mybir.dt.bfloat16
+U32 = mybir.dt.uint32
+U16 = mybir.dt.uint16
+U8 = mybir.dt.uint8
+FP8X4 = mybir.dt.float8_e4m3fn_x4
+
+P = 128
+LIST_COLS = C // 16
+
+HALF = T // 2
+
+
+def tile_routed_moe_kernel(tc, xT, w, offs, out):
+    nc = tc.nc
+    with ExitStack() as ctx:
+        keep = ctx.enter_context(tc.tile_pool(name="keep", bufs=1))
+        ring = ctx.enter_context(tc.tile_pool(name="ring", bufs=1))
+        psum = ctx.enter_context(tc.psum_pool(name="psum", bufs=1))
+
+        offsets = keep.tile([P, T // 16], U16, name="offsets")
+
+        x_rows = xT.rearrange("(p u e) n -> p u e n", u=2, e=2)
+        raw = []
+        for u in range(2):
+            raw_u = []
+            for h in range(2):
+                raw_uh = keep.tile([P, 2, HALF], F32, name="raw%d%d" % (u, h))
+                nc.sync.dma_start(raw_uh[:], x_rows[:, u, :, h * HALF : (h + 1) * HALF])
+                raw_u.append(raw_uh)
+            raw.append(raw_u)
+            if u == 0:
+                nc.sync.dma_start(offsets[:], offs)
+        w_rows = w.rearrange("e (p j) n -> e p j n", j=4)
+        w_raw = []
+        for e in range(E):
+            w_raw_e = keep.tile([P, 4, N], F32, name="w_raw%d" % e)
+            nc.sync.dma_start(w_raw_e[:], w_rows[e])
+            w_raw.append(w_raw_e)
+
+        pairs = [keep.tile([P, T, 2], BF16, name="pairs%d" % u) for u in range(2)]
+        ahead = keep.tile([P, C, 2], BF16, name="ahead")
+        x_codes = [keep.tile([P, C], U32, name="x_codes%d" % e, align_bytes=64) for e in range(E)]
+        x_scales = [keep.tile([P, C], U8, name="x_scales%d" % e, align_bytes=64) for e in range(E)]
+        w_grouped = [keep.tile([P, N, 4], BF16, name="w_grouped%d" % e, align_bytes=64) for e in range(E)]
+        w_codes = [keep.tile([P, N], U32, name="w_codes%d" % e, align_bytes=64) for e in range(E)]
+        w_scales = [keep.tile([P, N], U8, name="w_scales%d" % e, align_bytes=64) for e in range(E)]
+        acc = [psum.tile([P, C], F32, name="acc%d" % e) for e in range(E)]
+        sums = [keep.tile([P, C], F32, name="sums%d" % e) for e in range(E)]
+        result = keep.tile([P, T], F32, name="result")
+
+        def cast_pairs(u, h):
+            dst = pairs[u][:, h * HALF : (h + 1) * HALF, :]
+            src = raw[u][h][:].rearrange("p e n -> p n e")
+            if u == 0:
+                nc.vector.tensor_copy(out=dst, in_=src)
+            else:
+                nc.scalar.copy(out=dst, in_=src)
+
+        def gather(e, u, dst):
+            window = pairs[u][:].rearrange("p n e -> p (n e)").bitcast(U32)
+            nc.vector.tensor_copy(
+                out=dst,
+                in_=window.indirect(offsets[:, e * LIST_COLS : (e + 1) * LIST_COLS]),
+            )
+
+        def words_of(grouped, u):
+            return grouped[:].rearrange("p c t -> p (c t)").bitcast(U32).rearrange("p (c u) -> p c u", u=2)[:, :, u]
+
+        def interleave_w(e):
+            nc.scalar.copy(out=w_grouped[e][:], in_=w_raw[e][:].rearrange("p j n -> p n j"))
+
+        def quantize_w(e):
+            nc.vector.quantize_mx(
+                out=w_codes[e][:].bitcast(FP8X4),
+                scales=w_scales[e][:],
+                in_=w_grouped[e][:].rearrange("p n j -> p (n j)"),
+            )
+
+        def quantize_x(e, grouped):
+            nc.vector.quantize_mx(
+                out=x_codes[e][:].bitcast(FP8X4),
+                scales=x_scales[e][:],
+                in_=grouped[:].rearrange("p c t -> p (c t)"),
+            )
+
+        def multiply(e):
+            nc.tensor.matmul_mx(
+                out=acc[e][:],
+                lhsT=w_codes[e][:].bitcast(FP8X4),
+                lhsT_scale=w_scales[e][:],
+                rhs=x_codes[e][:].bitcast(FP8X4),
+                rhs_scale=x_scales[e][:],
+                start=True,
+                stop=True,
+            )
+            nc.scalar.copy(out=sums[e][:], in_=acc[e][:])
+
+        def scatter(e):
+            nc.vector.tensor_copy(
+                out=result[:].indirect(offsets[:, e * LIST_COLS : (e + 1) * LIST_COLS]),
+                in_=sums[e][:],
+            )
+
+        cast_pairs(0, 0)
+        cast_pairs(0, 1)
+        grouped0 = ring.tile([P, C, 4], BF16, name="grouped", align_bytes=64)
+        gather(0, 0, words_of(grouped0, 0))
+        gather(1, 0, ahead[:].rearrange("p c t -> p (c t)").bitcast(U32))
+        cast_pairs(1, 0)
+        cast_pairs(1, 1)
+        interleave_w(0)
+        interleave_w(1)
+        gather(0, 1, words_of(grouped0, 1))
+        quantize_w(0)
+        quantize_x(0, grouped0)
+        multiply(0)
+        grouped1 = ring.tile([P, C, 4], BF16, name="grouped", align_bytes=64)
+        nc.scalar.copy(out=grouped1[:, :, 0:2], in_=ahead[:])
+        gather(1, 1, words_of(grouped1, 1))
+        quantize_w(1)
+        quantize_x(1, grouped1)
+        multiply(1)
+        scatter(0)
+        scatter(1)
+
+        nc.sync.dma_start(out, result[:])

@@ -57,8 +57,8 @@ def tile_routed_moe_kernel(tc, xT, w, offs, out):
         result = keep.tile([P, T], F32, name="result")
 
         def cast_pairs(u, h):
-            dst = pairs[u][:, h * HALF : (h + 1) * HALF, :]
-            src = raw[u][h][:].rearrange("p e n -> p n e")
+            dst = pairs[u][:, h * HALF : (h + 1) * HALF, :].rearrange("p (c i) e -> p c e i", i=4)
+            src = raw[u][h][:].rearrange("p e (c i) -> p c e i", i=4)
             if u == 0:
                 nc.vector.tensor_copy(out=dst, in_=src)
             else:
@@ -75,7 +75,10 @@ def tile_routed_moe_kernel(tc, xT, w, offs, out):
             return grouped[:].rearrange("p c t -> p (c t)").bitcast(U32).rearrange("p (c u) -> p c u", u=2)[:, :, u]
 
         def interleave_w(e):
-            nc.scalar.copy(out=w_grouped[e][:], in_=w_raw[e][:].rearrange("p j n -> p n j"))
+            nc.scalar.copy(
+                out=w_grouped[e][:].rearrange("p (c i) j -> p c j i", i=4),
+                in_=w_raw[e][:].rearrange("p j (c i) -> p c j i", i=4),
+            )
 
         def quantize_w(e):
             nc.vector.quantize_mx(

@@ -16,13 +16,14 @@ P = 128
 LIST_COLS = C // 16
 
 HALF = T // 2
+PADDED = 768
+AGAIN = 32
 
 
 def tile_routed_moe_kernel(tc, xT, w, offs, out):
     nc = tc.nc
     with ExitStack() as ctx:
         keep = ctx.enter_context(tc.tile_pool(name="keep", bufs=1))
-        ring = ctx.enter_context(tc.tile_pool(name="ring", bufs=1))
         psum = ctx.enter_context(tc.psum_pool(name="psum", bufs=1))
 
         offsets = keep.tile([P, T // 16], U16, name="offsets")
@@ -45,8 +46,8 @@ def tile_routed_moe_kernel(tc, xT, w, offs, out):
             nc.sync.dma_start(w_raw_e[:], w_rows[e])
             w_raw.append(w_raw_e)
 
-        pairs = [keep.tile([P, T, 2], BF16, name="pairs%d" % u) for u in range(2)]
-        ahead = keep.tile([P, C, 2], BF16, name="ahead")
+        pairs = [keep.tile([P, (PADDED, T)[u], 2], BF16, name="pairs%d" % u) for u in range(2)]
+        grouped = keep.tile([P, E * C, 4], BF16, name="grouped", align_bytes=64)
         x_codes = [keep.tile([P, C], U32, name="x_codes%d" % e, align_bytes=64) for e in range(E)]
         x_scales = [keep.tile([P, C], U8, name="x_scales%d" % e, align_bytes=64) for e in range(E)]
         w_grouped = [keep.tile([P, N, 4], BF16, name="w_grouped%d" % e, align_bytes=64) for e in range(E)]
@@ -64,15 +65,14 @@ def tile_routed_moe_kernel(tc, xT, w, offs, out):
             else:
                 nc.scalar.copy(out=dst, in_=src)
 
-        def gather(e, u, dst):
+        words = grouped[:].rearrange("p c t -> p (c t)").bitcast(U32).rearrange("p (c u) -> p u c", u=2)
+
+        def gather(u, first, last):
             window = pairs[u][:].rearrange("p n e -> p (n e)").bitcast(U32)
             nc.vector.tensor_copy(
-                out=dst,
-                in_=window.indirect(offsets[:, e * LIST_COLS : (e + 1) * LIST_COLS]),
+                out=words[:, u, first:last],
+                in_=window.indirect(offsets[:, first // 16 : last // 16]),
             )
-
-        def words_of(grouped, u):
-            return grouped[:].rearrange("p c t -> p (c t)").bitcast(U32).rearrange("p (c u) -> p c u", u=2)[:, :, u]
 
         def interleave_w(e):
             nc.scalar.copy(
@@ -87,11 +87,11 @@ def tile_routed_moe_kernel(tc, xT, w, offs, out):
                 in_=w_grouped[e][:].rearrange("p n j -> p (n j)"),
             )
 
-        def quantize_x(e, grouped):
+        def quantize_x(e, first, last):
             nc.vector.quantize_mx(
-                out=x_codes[e][:].bitcast(FP8X4),
-                scales=x_scales[e][:],
-                in_=grouped[:].rearrange("p c t -> p (c t)"),
+                out=x_codes[e][:, first:last].bitcast(FP8X4),
+                scales=x_scales[e][:, first:last],
+                in_=grouped[:, e * C + first : e * C + last, :].rearrange("p c t -> p (c t)"),
             )
 
         def multiply(e):
@@ -114,22 +114,20 @@ def tile_routed_moe_kernel(tc, xT, w, offs, out):
 
         cast_pairs(0, 0)
         cast_pairs(0, 1)
-        grouped0 = ring.tile([P, C, 4], BF16, name="grouped", align_bytes=64)
-        gather(0, 0, words_of(grouped0, 0))
-        gather(1, 0, ahead[:].rearrange("p c t -> p (c t)").bitcast(U32))
+        gather(0, 0, E * C)
         cast_pairs(1, 0)
         cast_pairs(1, 1)
         interleave_w(0)
         interleave_w(1)
-        gather(0, 1, words_of(grouped0, 1))
+        gather(1, C // 2, C)
+        gather(1, 0, C // 2)
         quantize_w(0)
-        quantize_x(0, grouped0)
+        quantize_x(0, C // 2, C)
+        quantize_x(0, 0, C // 2)
         multiply(0)
-        grouped1 = ring.tile([P, C, 4], BF16, name="grouped", align_bytes=64)
-        nc.scalar.copy(out=grouped1[:, :, 0:2], in_=ahead[:])
-        gather(1, 1, words_of(grouped1, 1))
+        gather(1, C - AGAIN, E * C)
         quantize_w(1)
-        quantize_x(1, grouped1)
+        quantize_x(1, 0, C)
         multiply(1)
         scatter(0)
         scatter(1)

@@ -24,6 +24,7 @@ def tile_routed_moe_kernel(tc, xT, w, offs, out):
     nc = tc.nc
     with ExitStack() as ctx:
         keep = ctx.enter_context(tc.tile_pool(name="keep", bufs=1))
+        ring = ctx.enter_context(tc.tile_pool(name="ring", bufs=1))
         psum = ctx.enter_context(tc.psum_pool(name="psum", bufs=1))
 
         offsets = keep.tile([P, T // 16], U16, name="offsets")
@@ -42,13 +43,14 @@ def tile_routed_moe_kernel(tc, xT, w, offs, out):
         w_rows = w.rearrange("e (p j) n -> e p j n", j=4)
         w_raw = []
         for e in range(E):
-            w_raw_e = keep.tile([P, 4, N], F32, name="w_raw%d" % e)
+            pool = (ring, keep)[e]
+            w_raw_e = pool.tile([P, 4, N], F32, name=("turns", "w_raw1")[e], align_bytes=64)
             nc.sync.dma_start(w_raw_e[:], w_rows[e])
             w_raw.append(w_raw_e)
 
         pairs = [keep.tile([P, (PADDED, T)[u], 2], BF16, name="pairs%d" % u) for u in range(2)]
         grouped = keep.tile([P, E * C, 4], BF16, name="grouped", align_bytes=64)
-        x_codes = [keep.tile([P, C], U32, name="x_codes%d" % e, align_bytes=64) for e in range(E)]
+        x_codes1 = keep.tile([P, C], U32, name="x_codes1", align_bytes=64)
         x_scales = [keep.tile([P, C], U8, name="x_scales%d" % e, align_bytes=64) for e in range(E)]
         w_grouped = [keep.tile([P, N, 4], BF16, name="w_grouped%d" % e, align_bytes=64) for e in range(E)]
         w_codes = [keep.tile([P, N], U32, name="w_codes%d" % e, align_bytes=64) for e in range(E)]
@@ -121,8 +123,10 @@ def tile_routed_moe_kernel(tc, xT, w, offs, out):
         interleave_w(1)
         gather(1, C // 2, C)
         gather(1, 0, C // 2)
-        quantize_w(0)
+        x_codes0 = ring.tile([P, C], U32, name="turns", align_bytes=64)
+        x_codes = [x_codes0, x_codes1]
         quantize_x(0, C // 2, C)
+        quantize_w(0)
         quantize_x(0, 0, C // 2)
         multiply(0)
         gather(1, C - AGAIN, E * C)

@@ -15,7 +15,7 @@ FP8X4 = mybir.dt.float8_e4m3fn_x4
 P = 128
 LIST_COLS = C // 16
 
-HALF = T // 2
+RANGES = (((0, 320), (320, 512)), ((0, 256), (256, 512)))
 PADDED = 768
 AGAIN = 32
 
@@ -33,9 +33,9 @@ def tile_routed_moe_kernel(tc, xT, w, offs, out):
         raw = []
         for u in range(2):
             raw_u = []
-            for h in range(2):
-                raw_uh = keep.tile([P, 2, HALF], F32, name="raw%d%d" % (u, h))
-                nc.sync.dma_start(raw_uh[:], x_rows[:, u, :, h * HALF : (h + 1) * HALF])
+            for h, (first, last) in enumerate(RANGES[u]):
+                raw_uh = keep.tile([P, 2, last - first], F32, name="raw%d%d" % (u, h))
+                nc.sync.dma_start(raw_uh[:], x_rows[:, u, :, first:last])
                 raw_u.append(raw_uh)
             raw.append(raw_u)
             if u == 0:
@@ -60,7 +60,7 @@ def tile_routed_moe_kernel(tc, xT, w, offs, out):
         result = keep.tile([P, T], F32, name="result")
 
         def cast_pairs(u, h):
-            dst = pairs[u][:, h * HALF : (h + 1) * HALF, :].rearrange("p (c i) e -> p c e i", i=4)
+            dst = pairs[u][:, slice(*RANGES[u][h]), :].rearrange("p (c i) e -> p c e i", i=4)
             src = raw[u][h][:].rearrange("p e (c i) -> p c e i", i=4)
             if u == 0:
                 nc.vector.tensor_copy(out=dst, in_=src)

from contextlib import ExitStack

import concourse.mybir as mybir

K, T, E, C, N = 512, 512, 2, 256, 128
FLOPS = 2 * K * N * E * C

F32 = mybir.dt.float32
BF16 = mybir.dt.bfloat16
U32 = mybir.dt.uint32
U16 = mybir.dt.uint16
U8 = mybir.dt.uint8
FP8X4 = mybir.dt.float8_e4m3fn_x4

P = 128
LIST_COLS = C // 16

RANGES = (((0, 320), (320, 512)), ((0, 256), (256, 512)))
PADDED = 768
AGAIN = 32


def tile_routed_moe_kernel(tc, xT, w, offs, out):
    nc = tc.nc
    with ExitStack() as ctx:
        keep = ctx.enter_context(tc.tile_pool(name="keep", bufs=1))
        ring = ctx.enter_context(tc.tile_pool(name="ring", bufs=1))
        psum = ctx.enter_context(tc.psum_pool(name="psum", bufs=1))

        offsets = keep.tile([P, T // 16], U16, name="offsets")

        x_rows = xT.rearrange("(p u e) n -> p u e n", u=2, e=2)
        raw = []
        for u in range(2):
            raw_u = []
            for h, (first, last) in enumerate(RANGES[u]):
                raw_uh = keep.tile([P, 2, last - first], F32, name="raw%d%d" % (u, h))
                nc.sync.dma_start(raw_uh[:], x_rows[:, u, :, first:last])
                raw_u.append(raw_uh)
            raw.append(raw_u)
            if u == 0:
                nc.sync.dma_start(offsets[:], offs)
        w_rows = w.rearrange("e (p j) n -> e p j n", j=4)
        w_raw = []
        for e in range(E):
            pool = (ring, keep)[e]
            w_raw_e = pool.tile([P, 4, N], F32, name=("turns", "w_raw1")[e], align_bytes=64)
            nc.sync.dma_start(w_raw_e[:], w_rows[e])
            w_raw.append(w_raw_e)

        pairs = [keep.tile([P, (PADDED, T)[u], 2], BF16, name="pairs%d" % u) for u in range(2)]
        grouped = keep.tile([P, E * C, 4], BF16, name="grouped", align_bytes=64)
        x_codes1 = keep.tile([P, C], U32, name="x_codes1", align_bytes=64)
        x_scales = [keep.tile([P, C], U8, name="x_scales%d" % e, align_bytes=64) for e in range(E)]
        w_grouped = [keep.tile([P, N, 4], BF16, name="w_grouped%d" % e, align_bytes=64) for e in range(E)]
        w_codes = [keep.tile([P, N], U32, name="w_codes%d" % e, align_bytes=64) for e in range(E)]
        w_scales = [keep.tile([P, N], U8, name="w_scales%d" % e, align_bytes=64) for e in range(E)]
        acc = [psum.tile([P, C], F32, name="acc%d" % e) for e in range(E)]
        sums = [keep.tile([P, C], F32, name="sums%d" % e) for e in range(E)]
        result = keep.tile([P, T], F32, name="result")

        def cast_pairs(u, h):
            dst = pairs[u][:, slice(*RANGES[u][h]), :].rearrange("p (c i) e -> p c e i", i=4)
            src = raw[u][h][:].rearrange("p e (c i) -> p c e i", i=4)
            if u == 0:
                nc.vector.tensor_copy(out=dst, in_=src)
            else:
                nc.scalar.copy(out=dst, in_=src)

        words = grouped[:].rearrange("p c t -> p (c t)").bitcast(U32).rearrange("p (c u) -> p u c", u=2)

        def gather(u, first, last):
            window = pairs[u][:].rearrange("p n e -> p (n e)").bitcast(U32)
            nc.vector.tensor_copy(
                out=words[:, u, first:last],
                in_=window.indirect(offsets[:, first // 16 : last // 16]),
            )

        def interleave_w(e):
            nc.scalar.copy(
                out=w_grouped[e][:].rearrange("p (c i) j -> p c j i", i=4),
                in_=w_raw[e][:].rearrange("p j (c i) -> p c j i", i=4),
            )

        def quantize_w(e):
            nc.vector.quantize_mx(
                out=w_codes[e][:].bitcast(FP8X4),
                scales=w_scales[e][:],
                in_=w_grouped[e][:].rearrange("p n j -> p (n j)"),
            )

        def quantize_x(e, first, last):
            nc.vector.quantize_mx(
                out=x_codes[e][:, first:last].bitcast(FP8X4),
                scales=x_scales[e][:, first:last],
                in_=grouped[:, e * C + first : e * C + last, :].rearrange("p c t -> p (c t)"),
            )

        def multiply(e):
            nc.tensor.matmul_mx(
                out=acc[e][:],
                lhsT=w_codes[e][:].bitcast(FP8X4),
                lhsT_scale=w_scales[e][:],
                rhs=x_codes[e][:].bitcast(FP8X4),
                rhs_scale=x_scales[e][:],
                start=True,
                stop=True,
            )
            nc.scalar.copy(out=sums[e][:], in_=acc[e][:])

        def scatter(e):
            nc.vector.tensor_copy(
                out=result[:].indirect(offsets[:, e * LIST_COLS : (e + 1) * LIST_COLS]),
                in_=sums[e][:],
            )

        cast_pairs(0, 0)
        cast_pairs(0, 1)
        gather(0, 0, E * C)
        cast_pairs(1, 0)
        cast_pairs(1, 1)
        interleave_w(0)
        interleave_w(1)
        gather(1, C // 2, C)
        gather(1, 0, C // 2)
        x_codes0 = ring.tile([P, C], U32, name="turns", align_bytes=64)
        x_codes = [x_codes0, x_codes1]
        quantize_x(0, C // 2, C)
        quantize_w(0)
        quantize_x(0, 0, C // 2)
        multiply(0)
        gather(1, C - AGAIN, E * C)
        quantize_w(1)
        quantize_x(1, 0, C)
        multiply(1)
        scatter(0)
        scatter(1)

        nc.sync.dma_start(out, result[:])
